import numpy as np
import ml_dtypes


def mxq(x, axis, fmt="e4m3"):
    dtype, down = {"e4m3": (ml_dtypes.float8_e4m3fn, 7), "e5m2": (ml_dtypes.float8_e5m2, 14)}[fmt]
    v = np.moveaxis(np.asarray(x, np.float32).astype(ml_dtypes.bfloat16).astype(np.float64), axis, -1)
    blocks = v.reshape(v.shape[:-1] + (-1, 32))
    amax = np.abs(blocks).max(-1, keepdims=True)
    byte = np.maximum(np.where(amax > 0, np.frexp(amax)[1] - 1 + 127, 0) - down, 1)
    scale = np.exp2(byte - 127.0)
    codes = (blocks / scale).astype(np.float32).astype(dtype).astype(np.float64)
    return np.moveaxis((codes * scale).reshape(v.shape), -1, axis)


WIDE = False


def mx_kscale(k):
    if not WIDE:
        return np.ones(k)
    levels = np.array([10, -10, 5, -5, 0])
    if k % 512:
        return np.exp2(np.random.permutation(np.resize(levels, k // 32))).repeat(32)
    a = np.empty((k // 512, 16))
    for p in range(k // 512):
        a[p, :8] = np.random.permutation(np.resize(levels, 8))
        for g in range(8):
            far = levels[np.abs(levels - a[p, g]) >= 10]
            a[p, g + 8] = far[np.random.randint(len(far))]
    return np.exp2(a.ravel()).repeat(32)


def f64(x):
    return np.asarray(x).astype(np.float64)


def striped(idx):
    return np.tile(idx.reshape(-1, 16).T, (8, 1)).astype(np.uint16)


def unstriped(offs):
    return offs[:16].T.reshape(-1).astype(np.int64)


def pack_weight(w):
    k, n = w.shape
    w = f64(np.asarray(w, np.float32).astype(ml_dtypes.bfloat16)).reshape(k // 32, 32, n)
    amax = np.abs(w).max(1)
    byte = np.clip(np.where(amax > 0, np.frexp(amax)[1] - 1 + 127 - 7, 1), 1, 254)
    scaled = (w * np.exp2(127.0 - byte)[:, None, :]).reshape(k, n).astype(np.float32)
    words = np.ascontiguousarray(scaled.reshape(k // 512, 128, 4, n).transpose(0, 1, 3, 2)).astype(ml_dtypes.float8_e4m3fn).view(np.uint8)
    return words, np.ascontiguousarray(byte.astype(np.uint8).reshape(k // 512, 16, n))


def unpack_weight(words, scales):
    g, p, n, _ = words.shape
    vals = np.ascontiguousarray(words).view(ml_dtypes.float8_e4m3fn).astype(np.float64) * np.repeat(np.exp2(scales.astype(np.float64) - 127.0), 8, axis=1)[..., None]
    return vals.transpose(0, 1, 3, 2).reshape(g * 512, n)


def sigmoid(v):
    return 1.0 / (1.0 + np.exp(-np.maximum(v, -700.0)))


K, T, S, N, H = 512, 2048, 512, 512, 512


def setup_inputs():
    n = np.random.standard_normal
    s = mx_kscale(K)[:, None]
    u = mx_kscale(S)
    packed_xT = pack_weight(n((K, T)) * s)
    return {
        "x_words": packed_xT[0],
        "x_scales": packed_xT[1],
        "wa": (n((K, H)) / np.sqrt(K) / s).astype(np.float32),
        "wb": (n((K, N)) / np.sqrt(K) / s).astype(np.float32),
        "sl": np.random.uniform(1.0, 2.0, (S, 1)).astype(np.float32),
        "th": (0.5 * n((S, 1))).astype(np.float32),
        "gt": (np.random.uniform(0.5, 1.5, (S, 1)) * u[:, None]).astype(np.float32),
        "gi": (np.random.uniform(0.5, 1.5, (S, 1)) / u[:, None]).astype(np.float32),
        "sl2": np.random.uniform(1.0, 2.0, (H, 1)).astype(np.float32),
        "th2": (0.5 * n((H, 1))).astype(np.float32),
        "sl3": np.random.uniform(1.0, 2.0, (H, 1)).astype(np.float32),
        "th3": (0.5 * n((H, 1))).astype(np.float32),
        "offs": striped(np.random.permutation(T)[:S]),
        "two": striped(np.random.permutation(T)[:S]),
        "n1": striped(np.random.permutation(H)),
        "n2": striped(np.random.permutation(H)),
        "n3": striped(np.random.permutation(N)),
        "n4": striped(np.random.permutation(N)),
    }


def reference(x_words, x_scales, wa, wb, sl, th, gt, gi, sl2, th2, sl3, th3, offs, two, n1, n2, n3, n4):
    xq = unpack_weight(x_words, x_scales)[:, unstriped(offs)]
    a = xq.T @ mxq(f64(wa), 0, "e4m3")
    sg = sigmoid(f64(sl) * (a[:, unstriped(n1)] - f64(th)))
    z = f64(gt) * (np.maximum(a * sg, 0.75 * a[:, unstriped(n2)]))
    x_two = unpack_weight(x_words, x_scales)[:, unstriped(two)]
    b = x_two.T @ mxq(f64(wb), 0, "e4m3")
    z2 = f64(gi) * b
    cv = 0.0625 * ((mxq(z, 0, "e4m3").T @ mxq(z2, 0, "e4m3")))
    sg2 = sigmoid(f64(sl2) * (cv[:, unstriped(n3)] - f64(th2)))
    sg3 = sigmoid(f64(sl3) * (f64(th3) - cv[:, unstriped(n4)]))
    return 2.0 * ((cv * sg2) * sg3)

@@ -1,0 +1,253 @@
+from contextlib import ExitStack
+
+import concourse.mybir as mybir
+
+K, T, S, N, H = 512, 2048, 512, 512, 512
+FLOPS = 2 * K * S * H + 2 * K * S * N + 2 * S * H * N
+
+F32 = mybir.dt.float32
+BF16 = mybir.dt.bfloat16
+I32 = mybir.dt.int32
+U32 = mybir.dt.uint32
+U16 = mybir.dt.uint16
+U8 = mybir.dt.uint8
+FP8X4 = mybir.dt.float8_e4m3fn_x4
+MULT = mybir.AluOpType.mult
+MAX = mybir.AluOpType.max
+SIGMOID = mybir.ActivationFunctionType.Sigmoid
+COPY = mybir.ActivationFunctionType.Copy
+
+P = 128
+PACK = 4
+HALF = 256
+LIST_ROWS = 16
+RUN = 4
+SPLIT = 176
+
+
+def tile_picked_momemoecr_none_p_kernel(
+    tc, x_words, x_scales, wa, wb, sl, th, gt, gi, sl2, th2, sl3, th3, offs, two, n1, n2, n3, n4, out
+):
+    nc = tc.nc
+    with ExitStack() as ctx:
+        lists = ctx.enter_context(tc.tile_pool(name="lists", bufs=1))
+        keep = ctx.enter_context(tc.tile_pool(name="keep", bufs=1))
+        psum = ctx.enter_context(tc.psum_pool(name="psum", bufs=1))
+
+        def load_list(name, src):
+            tile = lists.tile([P, S // LIST_ROWS], U16, name=name)
+            nc.sync.dma_start(tile[:], src)
+            return tile
+
+        def load_by_place(name, src):
+            tile = keep.tile([P, PACK], F32, name=name)
+            nc.sync.dma_start(tile[:], src.rearrange("(p j) o -> p (j o)", j=PACK))
+            return tile
+
+        def load_by_row(name, src):
+            tile = keep.tile([P, H // P], F32, name=name)
+            with nc.allow_non_contiguous_dma(reason="one value a partition and row tile"):
+                nc.sync.dma_start(tile[:], src.rearrange("(m p) o -> p (m o)", p=P))
+            return tile
+
+        def load_weight(name, src, c0, width):
+            tile = keep.tile([P, PACK, width], F32, name=name)
+            nc.sync.dma_start(tile[:], src.rearrange("(p j) c -> p j c", j=PACK)[:, :, c0 : c0 + width])
+            return tile
+
+        def entries(tile, e0, count):
+            return tile[:, e0 // LIST_ROWS : (e0 + count) // LIST_ROWS]
+
+        def planes(ap):
+            return ap.rearrange("p t (c i) -> p c t i", i=RUN)
+
+        def woven(ap):
+            return ap.rearrange("p (c i) t -> p c t i", i=RUN)
+
+        def quantize(codes, scales, values):
+            nc.vector.quantize_mx(out=codes.bitcast(FP8X4), scales=scales, in_=values.rearrange("p c t -> p (c t)"))
+
+        def dealt(tile):
+            return tile[:].rearrange("p (j m) -> p m j", j=PACK)
+
+        table_scales = keep.tile([P, T], U8, name="table_scales")
+        nc.vector.memset(table_scales[:].bitcast(I32), 0)
+        offs_sb = load_list("offs_sb", offs)
+        table_words = keep.tile([P, T], I32, name="table_words")
+        nc.sync.dma_start(table_words[:], x_words[0].rearrange("p c r -> p (c r)").bitcast(I32))
+        for r in range(4):
+            nc.scalar.dma_start(table_scales[r:P:32, :].bitcast(I32), x_scales[0, r:16:4, :].bitcast(I32))
+        warm_in = keep.tile([P, 1], F32, name="warm_in")
+        nc.vector.memset(warm_in[:], 0.0)
+        warm_out = keep.tile([P, 1], F32, name="warm_out")
+        nc.scalar.activation(warm_out[:], warm_in[:], SIGMOID)
+        two_sb = load_list("two_sb", two)
+        wa_raw = [load_weight(f"wa_raw{u}", wa, u * HALF, HALF) for u in range(2)]
+        sl_sb = load_by_place("sl_sb", sl)
+        th_sb = load_by_place("th_sb", th)
+        n1_sb = load_list("n1_sb", n1)
+        n2_sb = load_list("n2_sb", n2)
+        wb_raw = load_weight("wb_raw", wb, 0, N)
+        gi_sb = load_by_place("gi_sb", gi)
+        gt_sb = load_by_place("gt_sb", gt)
+        n3_sb = load_list("n3_sb", n3)
+        n4_sb = load_list("n4_sb", n4)
+        sl2_sb = load_by_row("sl2_sb", sl2)
+        th2_sb = load_by_row("th2_sb", th2)
+        sl3_sb = load_by_row("sl3_sb", sl3)
+        th3_sb = load_by_row("th3_sb", th3)
+
+        xa_scales = keep.tile([P, S], U8, name="xa_scales", align_bytes=64)
+        nc.vector.tensor_copy(dealt(xa_scales), table_scales[:].indirect(offs_sb[:]))
+        xa_words = keep.tile([P, S], U32, name="xa_words", align_bytes=64)
+        nc.vector.tensor_copy(dealt(xa_words), table_words[:].bitcast(U32).indirect(offs_sb[:]))
+
+        wa_codes = keep.tile([P, H], U32, name="wa_codes", align_bytes=64)
+        wa_scales = keep.tile([P, H], U8, name="wa_scales", align_bytes=64)
+        wa_bf0 = keep.tile([P, HALF, PACK], BF16, name="wa_bf0", align_bytes=64)
+        nc.scalar.copy(woven(wa_bf0[:]), planes(wa_raw[0][:]))
+        wa_bf1 = keep.tile([P, HALF, PACK], BF16, name="wa_bf1", tag="after_wa", align_bytes=64)
+        nc.vector.tensor_copy(woven(wa_bf1[:, :SPLIT, :]), planes(wa_raw[1][:, :, :SPLIT]))
+        nc.scalar.copy(woven(wa_bf1[:, SPLIT:, :]), planes(wa_raw[1][:, :, SPLIT:]))
+        quantize(wa_codes[:, :HALF], wa_scales[:, :HALF], wa_bf0[:])
+        quantize(wa_codes[:, HALF:], wa_scales[:, HALF:], wa_bf1[:])
+
+        xb_scales = keep.tile([P, S], U8, name="xb_scales", align_bytes=64)
+        nc.vector.tensor_copy(dealt(xb_scales), table_scales[:].indirect(two_sb[:]))
+        xb_words = keep.tile([P, S], U32, name="xb_words", tag="after_wa", align_bytes=64)
+        nc.vector.tensor_copy(dealt(xb_words), table_words[:].bitcast(U32).indirect(two_sb[:]))
+
+        bias1 = keep.tile([P, PACK], F32, name="bias1")
+        nc.vector.scalar_tensor_tensor(bias1[:], sl_sb[:], -1.0, th_sb[:], MULT, MULT)
+
+        a_sb = [keep.tile([P, H], F32, name=f"a_sb{j}") for j in range(PACK)]
+        sg = [keep.tile([P, PACK, HALF], F32, name=f"sg{u}") for u in range(2)]
+        other = [keep.tile([P, PACK, HALF], F32, name=f"other{u}") for u in range(2)]
+
+        def look_up_in_a(u, j):
+            nc.scalar.activation(
+                sg[u][:, j, :],
+                a_sb[j][:].indirect(entries(n1_sb, u * HALF, HALF)),
+                SIGMOID,
+                bias=bias1[:, j : j + 1],
+                scale=sl_sb[:, j : j + 1],
+            )
+            nc.scalar.activation(
+                other[u][:, j, :], a_sb[j][:].indirect(entries(n2_sb, u * HALF, HALF)), COPY, scale=0.75
+            )
+
+        for j in range(PACK):
+            cols = slice(j * P, (j + 1) * P)
+            bank = psum.tile([P, H], F32, name=f"a_ps{j}", tag=f"rows{j}")
+            nc.tensor.matmul_mx(
+                out=bank[:],
+                lhsT=xa_words[:, cols].bitcast(FP8X4),
+                lhsT_scale=xa_scales[:, cols],
+                rhs=wa_codes[:].bitcast(FP8X4),
+                rhs_scale=wa_scales[:],
+                start=True,
+                stop=True,
+            )
+            nc.scalar.copy(a_sb[j][:], bank[:])
+            look_up_in_a(0, j)
+        for j in range(PACK):
+            look_up_in_a(1, j)
+
+        wb_bf = keep.tile([P, N, PACK], BF16, name="wb_bf", tag="after_wb", align_bytes=64)
+        nc.vector.tensor_copy(woven(wb_bf[:]), planes(wb_raw[:]))
+        wb_codes = keep.tile([P, N], U32, name="wb_codes", align_bytes=64)
+        wb_scales = keep.tile([P, N], U8, name="wb_scales", align_bytes=64)
+        quantize(wb_codes[:], wb_scales[:], wb_bf[:])
+        z2_bf = keep.tile([P, N, PACK], BF16, name="z2_bf", align_bytes=64)
+        for n in range(N // P):
+            cols = slice(n * P, (n + 1) * P)
+            bank = psum.tile([P, PACK, P], F32, name=f"b_ps{n}")
+            for j in range(PACK):
+                places = slice(j * P, (j + 1) * P)
+                nc.tensor.matmul_mx(
+                    out=bank[:, j, :],
+                    lhsT=xb_words[:, places].bitcast(FP8X4),
+                    lhsT_scale=xb_scales[:, places],
+                    rhs=wb_codes[:, cols].bitcast(FP8X4),
+                    rhs_scale=wb_scales[:, cols],
+                    start=True,
+                    stop=True,
+                )
+            nc.vector.tensor_tensor(
+                z2_bf[:, cols, :],
+                bank[:].rearrange("p j c -> p c j"),
+                gi_sb[:].unsqueeze(1).to_broadcast([P, P, PACK]),
+                MULT,
+            )
+        z2_codes = keep.tile([P, N], U32, name="z2_codes", align_bytes=64)
+        z2_scales = keep.tile([P, N], U8, name="z2_scales", align_bytes=64)
+        quantize(z2_codes[:], z2_scales[:], z2_bf[:])
+
+        bias2 = keep.tile([P, H // P], F32, name="bias2")
+        nc.vector.scalar_tensor_tensor(bias2[:], sl2_sb[:], -1.0, th2_sb[:], MULT, MULT)
+        scale3 = keep.tile([P, H // P], F32, name="scale3")
+        nc.vector.tensor_scalar(scale3[:], sl3_sb[:], -1.0, None, MULT)
+        bias3 = keep.tile([P, H // P], F32, name="bias3")
+        nc.vector.tensor_tensor(bias3[:], sl3_sb[:], th3_sb[:], MULT)
+
+        cv_sb = []
+        for u in range(2):
+            tag = "after_wb" if u == 0 else "after_z1"
+            gated = keep.tile([P, PACK, HALF], F32, name=f"gated{u}", tag=tag, align_bytes=64)
+            for j in range(PACK):
+                nc.vector.tensor_tensor(gated[:, j, :], a_sb[j][:, u * HALF : (u + 1) * HALF], sg[u][:, j, :], MULT)
+            tiles = [2 * u, 2 * u + 1]
+            larger, z_bf, z_codes, z_scales = {}, {}, {}, {}
+            for m in tiles:
+                part = slice((m % 2) * P, (m % 2 + 1) * P)
+                larger[m] = keep.tile([P, PACK, P], F32, name=f"larger{m}")
+                nc.vector.tensor_tensor(larger[m][:], gated[:, :, part], other[u][:, :, part], MAX)
+            for m in tiles:
+                z_bf[m] = keep.tile([P, P, PACK], BF16, name=f"z_bf{m}", tag=f"after_z{m}", align_bytes=64)
+                nc.vector.tensor_tensor(
+                    woven(z_bf[m][:]),
+                    planes(larger[m][:]),
+                    gt_sb[:].unsqueeze(1).unsqueeze(3).to_broadcast([P, P // RUN, PACK, RUN]),
+                    MULT,
+                )
+            for m in tiles:
+                z_codes[m] = keep.tile([P, P], U32, name=f"z_codes{m}", align_bytes=64)
+                z_scales[m] = keep.tile([P, P], U8, name=f"z_scales{m}", align_bytes=64)
+                quantize(z_codes[m][:], z_scales[m][:], z_bf[m][:])
+            for m in tiles:
+                bank = psum.tile([P, N], F32, name=f"cv_ps{m}", tag=f"rows{m}")
+                nc.tensor.matmul_mx(
+                    out=bank[:],
+                    lhsT=z_codes[m][:].bitcast(FP8X4),
+                    lhsT_scale=z_scales[m][:],
+                    rhs=z2_codes[:].bitcast(FP8X4),
+                    rhs_scale=z2_scales[:],
+                    start=True,
+                    stop=True,
+                )
+                cv_m = keep.tile([P, N], F32, name=f"cv_sb{m}")
+                nc.vector.tensor_scalar(cv_m[:], bank[:], 0.0625, None, MULT)
+                cv_sb.append(cv_m)
+
+        last = H // P - 1
+        for m in range(H // P):
+            row = slice(m, m + 1)
+            sg2 = keep.tile([P, N], F32, name=f"sg2_{m}")
+            sg3 = keep.tile([P, N], F32, name=f"sg3_{m}")
+            for gate, places, scale, bias in ((sg2, n3_sb, sl2_sb, bias2), (sg3, n4_sb, scale3, bias3)):
+                for c0 in range(0, N, HALF):
+                    nc.scalar.activation(
+                        gate[:, c0 : c0 + HALF],
+                        cv_sb[m][:].indirect(entries(places, c0, HALF)),
+                        SIGMOID,
+                        bias=bias[:, row],
+                        scale=scale[:, row],
+                    )
+            twice = keep.tile([P, N], F32, name=f"twice{m}", tag=f"after_z{3 - m % 2}", align_bytes=64)
+            nc.vector.scalar_tensor_tensor(twice[:], cv_sb[m][:], 2.0, sg2[:], MULT, MULT)
+            width = HALF if m == last else N
+            for c0 in range(0, N, width):
+                cols = slice(c0, c0 + width)
+                result = keep.tile([P, width], F32, name=f"result{m}_{c0}")
+                nc.vector.tensor_tensor(result[:], twice[:, cols], sg3[:, cols], MULT)
+                nc.sync.dma_start(out[m * P : (m + 1) * P, cols], result[:])

@@ -1,6 +1,7 @@
 from contextlib import ExitStack
 
 import concourse.mybir as mybir
+from concourse.masks import make_identity
 
 K, T, S, N, H = 512, 2048, 512, 512, 512
 FLOPS = 2 * K * S * H + 2 * K * S * N + 2 * S * H * N
@@ -22,7 +23,7 @@ PACK = 4
 HALF = 256
 LIST_ROWS = 16
 RUN = 4
-SPLIT = 176
+GROUP = 8
 
 
 def tile_picked_momemoecr_none_p_kernel(
@@ -37,11 +38,6 @@ def tile_picked_momemoecr_none_p_kernel(
         def load_list(name, src):
             tile = lists.tile([P, S // LIST_ROWS], U16, name=name)
             nc.sync.dma_start(tile[:], src)
-            return tile
-
-        def load_by_place(name, src):
-            tile = keep.tile([P, PACK], F32, name=name)
-            nc.sync.dma_start(tile[:], src.rearrange("(p j) o -> p (j o)", j=PACK))
             return tile
 
         def load_by_row(name, src):
@@ -68,28 +64,32 @@ def tile_picked_momemoecr_none_p_kernel(
             nc.vector.quantize_mx(out=codes.bitcast(FP8X4), scales=scales, in_=values.rearrange("p c t -> p (c t)"))
 
         def dealt(tile):
-            return tile[:].rearrange("p (j m) -> p m j", j=PACK)
+            return tile[:].rearrange("p (j q r) -> p q j r", j=PACK, r=GROUP)
 
         table_scales = keep.tile([P, T], U8, name="table_scales")
         nc.vector.memset(table_scales[:].bitcast(I32), 0)
-        offs_sb = load_list("offs_sb", offs)
-        table_words = keep.tile([P, T], I32, name="table_words")
-        nc.sync.dma_start(table_words[:], x_words[0].rearrange("p c r -> p (c r)").bitcast(I32))
-        for r in range(4):
-            nc.scalar.dma_start(table_scales[r:P:32, :].bitcast(I32), x_scales[0, r:16:4, :].bitcast(I32))
         warm_in = keep.tile([P, 1], F32, name="warm_in")
         nc.vector.memset(warm_in[:], 0.0)
         warm_out = keep.tile([P, 1], F32, name="warm_out")
         nc.scalar.activation(warm_out[:], warm_in[:], SIGMOID)
+        offs_sb = load_list("offs_sb", offs)
         two_sb = load_list("two_sb", two)
-        wa_raw = [load_weight(f"wa_raw{u}", wa, u * HALF, HALF) for u in range(2)]
-        sl_sb = load_by_place("sl_sb", sl)
-        th_sb = load_by_place("th_sb", th)
+        wa_raw = [load_weight("wa_raw0", wa, 0, HALF)]
+        for r in range(4):
+            nc.sync.dma_start(table_scales[r:P:32, :].bitcast(I32), x_scales[0, r:16:4, :].bitcast(I32))
+        wa_raw.append(load_weight("wa_raw1", wa, HALF, HALF))
+        table_words = keep.tile([P, T], I32, name="table_words")
+        nc.sync.dma_start(table_words[:], x_words[0].rearrange("p c r -> p (c r)").bitcast(I32))
+        place_rows = keep.tile([P, P], F32, name="place_rows")
+        nc.gpsimd.memset(place_rows[:], 0.0)
+        for v, src in enumerate((sl, th, gt, gi)):
+            nc.sync.dma_start(
+                place_rows[PACK * v : PACK * (v + 1), :].rearrange("j (q r) -> j q r", r=GROUP),
+                src.rearrange("(q j r) o -> j q (r o)", j=PACK, r=GROUP),
+            )
         n1_sb = load_list("n1_sb", n1)
         n2_sb = load_list("n2_sb", n2)
         wb_raw = load_weight("wb_raw", wb, 0, N)
-        gi_sb = load_by_place("gi_sb", gi)
-        gt_sb = load_by_place("gt_sb", gt)
         n3_sb = load_list("n3_sb", n3)
         n4_sb = load_list("n4_sb", n4)
         sl2_sb = load_by_row("sl2_sb", sl2)
@@ -99,26 +99,26 @@ def tile_picked_momemoecr_none_p_kernel(
 
         xa_scales = keep.tile([P, S], U8, name="xa_scales", align_bytes=64)
         nc.vector.tensor_copy(dealt(xa_scales), table_scales[:].indirect(offs_sb[:]))
-        xa_words = keep.tile([P, S], U32, name="xa_words", align_bytes=64)
-        nc.vector.tensor_copy(dealt(xa_words), table_words[:].bitcast(U32).indirect(offs_sb[:]))
-
         wa_codes = keep.tile([P, H], U32, name="wa_codes", align_bytes=64)
         wa_scales = keep.tile([P, H], U8, name="wa_scales", align_bytes=64)
-        wa_bf0 = keep.tile([P, HALF, PACK], BF16, name="wa_bf0", align_bytes=64)
-        nc.scalar.copy(woven(wa_bf0[:]), planes(wa_raw[0][:]))
-        wa_bf1 = keep.tile([P, HALF, PACK], BF16, name="wa_bf1", tag="after_wa", align_bytes=64)
-        nc.vector.tensor_copy(woven(wa_bf1[:, :SPLIT, :]), planes(wa_raw[1][:, :, :SPLIT]))
-        nc.scalar.copy(woven(wa_bf1[:, SPLIT:, :]), planes(wa_raw[1][:, :, SPLIT:]))
-        quantize(wa_codes[:, :HALF], wa_scales[:, :HALF], wa_bf0[:])
-        quantize(wa_codes[:, HALF:], wa_scales[:, HALF:], wa_bf1[:])
-
+        wa_bf = keep.tile([P, H, PACK], BF16, name="wa_bf", align_bytes=64)
+        for u in range(2):
+            nc.scalar.copy(woven(wa_bf[:, u * HALF : (u + 1) * HALF, :]), planes(wa_raw[u][:]))
+        quantize(wa_codes[:], wa_scales[:], wa_bf[:])
+        xa_words = keep.tile([P, S], U32, name="xa_words", align_bytes=64)
+        nc.vector.tensor_copy(dealt(xa_words), table_words[:].bitcast(U32).indirect(offs_sb[:]))
         xb_scales = keep.tile([P, S], U8, name="xb_scales", align_bytes=64)
         nc.vector.tensor_copy(dealt(xb_scales), table_scales[:].indirect(two_sb[:]))
-        xb_words = keep.tile([P, S], U32, name="xb_words", tag="after_wa", align_bytes=64)
-        nc.vector.tensor_copy(dealt(xb_words), table_words[:].bitcast(U32).indirect(two_sb[:]))
 
+        identity = keep.tile([P, P], F32, name="identity")
+        make_identity(nc, identity[:])
+        turned = psum.tile([P, P], F32, name="turned", tag="b_ps0")
+        nc.tensor.transpose(turned[:], place_rows[:], identity[:])
+        by_place = keep.tile([P, 4 * PACK], F32, name="by_place")
+        nc.scalar.copy(by_place[:], turned[:, : 4 * PACK])
+        sl_sb, th_sb, gt_sb, gi_sb = [by_place[:, PACK * v : PACK * (v + 1)] for v in range(4)]
         bias1 = keep.tile([P, PACK], F32, name="bias1")
-        nc.vector.scalar_tensor_tensor(bias1[:], sl_sb[:], -1.0, th_sb[:], MULT, MULT)
+        nc.vector.scalar_tensor_tensor(bias1[:], sl_sb, -1.0, th_sb, MULT, MULT)
 
         a_sb = [keep.tile([P, H], F32, name=f"a_sb{j}") for j in range(PACK)]
         sg = [keep.tile([P, PACK, HALF], F32, name=f"sg{u}") for u in range(2)]
@@ -153,6 +153,8 @@ def tile_picked_momemoecr_none_p_kernel(
         for j in range(PACK):
             look_up_in_a(1, j)
 
+        xb_words = keep.tile([P, S], U32, name="xb_words", align_bytes=64)
+        nc.vector.tensor_copy(dealt(xb_words), table_words[:].bitcast(U32).indirect(two_sb[:]))
         wb_bf = keep.tile([P, N, PACK], BF16, name="wb_bf", tag="after_wb", align_bytes=64)
         nc.vector.tensor_copy(woven(wb_bf[:]), planes(wb_raw[:]))
         wb_codes = keep.tile([P, N], U32, name="wb_codes", align_bytes=64)
@@ -161,7 +163,7 @@ def tile_picked_momemoecr_none_p_kernel(
         z2_bf = keep.tile([P, N, PACK], BF16, name="z2_bf", align_bytes=64)
         for n in range(N // P):
             cols = slice(n * P, (n + 1) * P)
-            bank = psum.tile([P, PACK, P], F32, name=f"b_ps{n}")
+            bank = psum.tile([P, PACK, P], F32, name=f"b_ps{n}", tag=f"b_ps{n}")
             for j in range(PACK):
                 places = slice(j * P, (j + 1) * P)
                 nc.tensor.matmul_mx(
@@ -176,7 +178,7 @@ def tile_picked_momemoecr_none_p_kernel(
             nc.vector.tensor_tensor(
                 z2_bf[:, cols, :],
                 bank[:].rearrange("p j c -> p c j"),
-                gi_sb[:].unsqueeze(1).to_broadcast([P, P, PACK]),
+                gi_sb.unsqueeze(1).to_broadcast([P, P, PACK]),
                 MULT,
             )
         z2_codes = keep.tile([P, N], U32, name="z2_codes", align_bytes=64)
@@ -191,61 +193,64 @@ def tile_picked_momemoecr_none_p_kernel(
         nc.vector.tensor_tensor(bias3[:], sl3_sb[:], th3_sb[:], MULT)
 
         cv_sb = []
-        for u in range(2):
-            tag = "after_wb" if u == 0 else "after_z1"
-            gated = keep.tile([P, PACK, HALF], F32, name=f"gated{u}", tag=tag, align_bytes=64)
-            for j in range(PACK):
-                nc.vector.tensor_tensor(gated[:, j, :], a_sb[j][:, u * HALF : (u + 1) * HALF], sg[u][:, j, :], MULT)
-            tiles = [2 * u, 2 * u + 1]
-            larger, z_bf, z_codes, z_scales = {}, {}, {}, {}
-            for m in tiles:
-                part = slice((m % 2) * P, (m % 2 + 1) * P)
-                larger[m] = keep.tile([P, PACK, P], F32, name=f"larger{m}")
-                nc.vector.tensor_tensor(larger[m][:], gated[:, :, part], other[u][:, :, part], MAX)
-            for m in tiles:
-                z_bf[m] = keep.tile([P, P, PACK], BF16, name=f"z_bf{m}", tag=f"after_z{m}", align_bytes=64)
-                nc.vector.tensor_tensor(
-                    woven(z_bf[m][:]),
-                    planes(larger[m][:]),
-                    gt_sb[:].unsqueeze(1).unsqueeze(3).to_broadcast([P, P // RUN, PACK, RUN]),
-                    MULT,
-                )
-            for m in tiles:
-                z_codes[m] = keep.tile([P, P], U32, name=f"z_codes{m}", align_bytes=64)
-                z_scales[m] = keep.tile([P, P], U8, name=f"z_scales{m}", align_bytes=64)
-                quantize(z_codes[m][:], z_scales[m][:], z_bf[m][:])
-            for m in tiles:
-                bank = psum.tile([P, N], F32, name=f"cv_ps{m}", tag=f"rows{m}")
-                nc.tensor.matmul_mx(
-                    out=bank[:],
-                    lhsT=z_codes[m][:].bitcast(FP8X4),
-                    lhsT_scale=z_scales[m][:],
-                    rhs=z2_codes[:].bitcast(FP8X4),
-                    rhs_scale=z2_scales[:],
-                    start=True,
-                    stop=True,
-                )
-                cv_m = keep.tile([P, N], F32, name=f"cv_sb{m}")
-                nc.vector.tensor_scalar(cv_m[:], bank[:], 0.0625, None, MULT)
-                cv_sb.append(cv_m)
+        windows = [keep.tile([P, 2 * N], F32, name=f"cv_window{m}") for m in range(H // P)]
+        for window in windows:
+            nc.gpsimd.memset(window[:, N:], 0.0)
+        for m in range(H // P):
+            u, c0 = divmod(m * P, HALF)
+            part = slice(c0, c0 + P)
+            if c0 == 0:
+                tag = "after_wb" if u == 0 else "after_z1"
+                gated = keep.tile([P, PACK, HALF], F32, name=f"gated{u}", tag=tag, align_bytes=64)
+                for j in range(PACK):
+                    nc.vector.tensor_tensor(
+                        gated[:, j, :], a_sb[j][:, u * HALF : (u + 1) * HALF], sg[u][:, j, :], MULT
+                    )
+            larger = keep.tile([P, PACK, P], F32, name=f"larger{m}")
+            nc.vector.tensor_tensor(larger[:], gated[:, :, part], other[u][:, :, part], MAX)
+            z_bf = keep.tile([P, P, PACK], BF16, name=f"z_bf{m}", tag=f"after_z{m}", align_bytes=64)
+            nc.vector.tensor_tensor(
+                woven(z_bf[:]),
+                planes(larger[:]),
+                gt_sb.unsqueeze(1).unsqueeze(3).to_broadcast([P, P // RUN, PACK, RUN]),
+                MULT,
+            )
+            z_codes = keep.tile([P, P], U32, name=f"z_codes{m}", tag=f"after_cv{m}", align_bytes=64)
+            z_scales = keep.tile([P, P], U8, name=f"z_scales{m}", align_bytes=64)
+            quantize(z_codes[:], z_scales[:], z_bf[:])
+            bank = psum.tile([P, N], F32, name=f"cv_ps{m}", tag=f"rows{m}")
+            nc.tensor.matmul_mx(
+                out=bank[:],
+                lhsT=z_codes[:].bitcast(FP8X4),
+                lhsT_scale=z_scales[:],
+                rhs=z2_codes[:].bitcast(FP8X4),
+                rhs_scale=z2_scales[:],
+                start=True,
+                stop=True,
+            )
+            cv_m = windows[m][:, :N]
+            nc.vector.tensor_scalar(cv_m, bank[:], 0.0625, None, MULT)
+            cv_sb.append(cv_m)
 
         last = H // P - 1
+        twice_tags = ["after_z3", "after_cv3", "after_z3", "after_cv3"]
         for m in range(H // P):
             row = slice(m, m + 1)
             sg2 = keep.tile([P, N], F32, name=f"sg2_{m}")
             sg3 = keep.tile([P, N], F32, name=f"sg3_{m}")
+            width = HALF if m == last else N
             for gate, places, scale, bias in ((sg2, n3_sb, sl2_sb, bias2), (sg3, n4_sb, scale3, bias3)):
-                for c0 in range(0, N, HALF):
+                step = width if gate is sg3 else N
+                for c0 in range(0, N, step):
                     nc.scalar.activation(
-                        gate[:, c0 : c0 + HALF],
-                        cv_sb[m][:].indirect(entries(places, c0, HALF)),
+                        gate[:, c0 : c0 + step],
+                        windows[m][:].indirect(entries(places, c0, step)),
                         SIGMOID,
                         bias=bias[:, row],
                         scale=scale[:, row],
                     )
-            twice = keep.tile([P, N], F32, name=f"twice{m}", tag=f"after_z{3 - m % 2}", align_bytes=64)
-            nc.vector.scalar_tensor_tensor(twice[:], cv_sb[m][:], 2.0, sg2[:], MULT, MULT)
-            width = HALF if m == last else N
+            twice = keep.tile([P, N], F32, name=f"twice{m}", tag=twice_tags[m], align_bytes=64)
+            nc.vector.scalar_tensor_tensor(twice[:], cv_sb[m], 2.0, sg2[:], MULT, MULT)
             for c0 in range(0, N, width):
                 cols = slice(c0, c0 + width)
                 result = keep.tile([P, width], F32, name=f"result{m}_{c0}")

@@ -24,6 +24,7 @@ HALF = 256
 LIST_ROWS = 16
 RUN = 4
 GROUP = 8
+SCALAR_BANKS = 2
 
 
 def tile_picked_momemoecr_none_p_kernel(
@@ -112,7 +113,7 @@ def tile_picked_momemoecr_none_p_kernel(
 
         identity = keep.tile([P, P], F32, name="identity")
         make_identity(nc, identity[:])
-        turned = psum.tile([P, P], F32, name="turned", tag="b_ps0")
+        turned = psum.tile([P, P], F32, name="turned", tag="rows0")
         nc.tensor.transpose(turned[:], place_rows[:], identity[:])
         by_place = keep.tile([P, 4 * PACK], F32, name="by_place")
         nc.scalar.copy(by_place[:], turned[:, : 4 * PACK])
@@ -137,18 +138,21 @@ def tile_picked_momemoecr_none_p_kernel(
             )
 
         for j in range(PACK):
-            cols = slice(j * P, (j + 1) * P)
+            places = slice(j * P, (j + 1) * P)
             bank = psum.tile([P, H], F32, name=f"a_ps{j}", tag=f"rows{j}")
             nc.tensor.matmul_mx(
                 out=bank[:],
-                lhsT=xa_words[:, cols].bitcast(FP8X4),
-                lhsT_scale=xa_scales[:, cols],
+                lhsT=xa_words[:, places].bitcast(FP8X4),
+                lhsT_scale=xa_scales[:, places],
                 rhs=wa_codes[:].bitcast(FP8X4),
                 rhs_scale=wa_scales[:],
                 start=True,
                 stop=True,
             )
-            nc.scalar.copy(a_sb[j][:], bank[:])
+            if j < SCALAR_BANKS:
+                nc.scalar.copy(a_sb[j][:], bank[:])
+            else:
+                nc.vector.tensor_copy(a_sb[j][:], bank[:])
             look_up_in_a(0, j)
         for j in range(PACK):
             look_up_in_a(1, j)
@@ -197,9 +201,9 @@ def tile_picked_momemoecr_none_p_kernel(
         for window in windows:
             nc.gpsimd.memset(window[:, N:], 0.0)
         for m in range(H // P):
-            u, c0 = divmod(m * P, HALF)
-            part = slice(c0, c0 + P)
-            if c0 == 0:
+            u, start = divmod(m * P, HALF)
+            part = slice(start, start + P)
+            if start == 0:
                 tag = "after_wb" if u == 0 else "after_z1"
                 gated = keep.tile([P, PACK, HALF], F32, name=f"gated{u}", tag=tag, align_bytes=64)
                 for j in range(PACK):
@@ -229,7 +233,10 @@ def tile_picked_momemoecr_none_p_kernel(
                 stop=True,
             )
             cv_m = windows[m][:, :N]
-            nc.vector.tensor_scalar(cv_m, bank[:], 0.0625, None, MULT)
+            if m < SCALAR_BANKS:
+                nc.scalar.activation(cv_m, bank[:], COPY, scale=0.0625)
+            else:
+                nc.vector.tensor_scalar(cv_m, bank[:], 0.0625, None, MULT)
             cv_sb.append(cv_m)
 
         last = H // P - 1
@@ -239,12 +246,12 @@ def tile_picked_momemoecr_none_p_kernel(
             sg2 = keep.tile([P, N], F32, name=f"sg2_{m}")
             sg3 = keep.tile([P, N], F32, name=f"sg3_{m}")
             width = HALF if m == last else N
-            for gate, places, scale, bias in ((sg2, n3_sb, sl2_sb, bias2), (sg3, n4_sb, scale3, bias3)):
+            for gate, feature_list, scale, bias in ((sg2, n3_sb, sl2_sb, bias2), (sg3, n4_sb, scale3, bias3)):
                 step = width if gate is sg3 else N
                 for c0 in range(0, N, step):
                     nc.scalar.activation(
                         gate[:, c0 : c0 + step],
-                        windows[m][:].indirect(entries(places, c0, step)),
+                        windows[m][:].indirect(entries(feature_list, c0, step)),
                         SIGMOID,
                         bias=bias[:, row],
                         scale=scale[:, row],

from contextlib import ExitStack

import concourse.mybir as mybir
from concourse.masks import make_identity

K, T, S, N, H = 512, 2048, 512, 512, 512
FLOPS = 2 * K * S * H + 2 * K * S * N + 2 * S * H * N

F32 = mybir.dt.float32
BF16 = mybir.dt.bfloat16
I32 = mybir.dt.int32
U32 = mybir.dt.uint32
U16 = mybir.dt.uint16
U8 = mybir.dt.uint8
FP8X4 = mybir.dt.float8_e4m3fn_x4
MULT = mybir.AluOpType.mult
MAX = mybir.AluOpType.max
SIGMOID = mybir.ActivationFunctionType.Sigmoid
COPY = mybir.ActivationFunctionType.Copy

P = 128
PACK = 4
HALF = 256
LIST_ROWS = 16
RUN = 4
GROUP = 8
SCALAR_BANKS = 2


def tile_picked_momemoecr_none_p_kernel(
    tc, x_words, x_scales, wa, wb, sl, th, gt, gi, sl2, th2, sl3, th3, offs, two, n1, n2, n3, n4, out
):
    nc = tc.nc
    with ExitStack() as ctx:
        lists = ctx.enter_context(tc.tile_pool(name="lists", bufs=1))
        keep = ctx.enter_context(tc.tile_pool(name="keep", bufs=1))
        psum = ctx.enter_context(tc.psum_pool(name="psum", bufs=1))

        def load_list(name, src):
            tile = lists.tile([P, S // LIST_ROWS], U16, name=name)
            nc.sync.dma_start(tile[:], src)
            return tile

        def load_by_row(name, src):
            tile = keep.tile([P, H // P], F32, name=name)
            with nc.allow_non_contiguous_dma(reason="one value a partition and row tile"):
                nc.sync.dma_start(tile[:], src.rearrange("(m p) o -> p (m o)", p=P))
            return tile

        def load_weight(name, src, c0, width):
            tile = keep.tile([P, PACK, width], F32, name=name)
            nc.sync.dma_start(tile[:], src.rearrange("(p j) c -> p j c", j=PACK)[:, :, c0 : c0 + width])
            return tile

        def entries(tile, e0, count):
            return tile[:, e0 // LIST_ROWS : (e0 + count) // LIST_ROWS]

        def planes(ap):
            return ap.rearrange("p t (c i) -> p c t i", i=RUN)

        def woven(ap):
            return ap.rearrange("p (c i) t -> p c t i", i=RUN)

        def quantize(codes, scales, values):
            nc.vector.quantize_mx(out=codes.bitcast(FP8X4), scales=scales, in_=values.rearrange("p c t -> p (c t)"))

        def dealt(tile):
            return tile[:].rearrange("p (j q r) -> p q j r", j=PACK, r=GROUP)

        table_scales = keep.tile([P, T], U8, name="table_scales")
        nc.vector.memset(table_scales[:].bitcast(I32), 0)
        warm_in = keep.tile([P, 1], F32, name="warm_in")
        nc.vector.memset(warm_in[:], 0.0)
        warm_out = keep.tile([P, 1], F32, name="warm_out")
        nc.scalar.activation(warm_out[:], warm_in[:], SIGMOID)
        offs_sb = load_list("offs_sb", offs)
        two_sb = load_list("two_sb", two)
        wa_raw = [load_weight("wa_raw0", wa, 0, HALF)]
        for r in range(4):
            nc.sync.dma_start(table_scales[r:P:32, :].bitcast(I32), x_scales[0, r:16:4, :].bitcast(I32))
        wa_raw.append(load_weight("wa_raw1", wa, HALF, HALF))
        table_words = keep.tile([P, T], I32, name="table_words")
        nc.sync.dma_start(table_words[:], x_words[0].rearrange("p c r -> p (c r)").bitcast(I32))
        place_rows = keep.tile([P, P], F32, name="place_rows")
        nc.gpsimd.memset(place_rows[:], 0.0)
        for v, src in enumerate((sl, th, gt, gi)):
            nc.sync.dma_start(
                place_rows[PACK * v : PACK * (v + 1), :].rearrange("j (q r) -> j q r", r=GROUP),
                src.rearrange("(q j r) o -> j q (r o)", j=PACK, r=GROUP),
            )
        n1_sb = load_list("n1_sb", n1)
        n2_sb = load_list("n2_sb", n2)
        wb_raw = load_weight("wb_raw", wb, 0, N)
        n3_sb = load_list("n3_sb", n3)
        n4_sb = load_list("n4_sb", n4)
        sl2_sb = load_by_row("sl2_sb", sl2)
        th2_sb = load_by_row("th2_sb", th2)
        sl3_sb = load_by_row("sl3_sb", sl3)
        th3_sb = load_by_row("th3_sb", th3)

        xa_scales = keep.tile([P, S], U8, name="xa_scales", align_bytes=64)
        nc.vector.tensor_copy(dealt(xa_scales), table_scales[:].indirect(offs_sb[:]))
        wa_codes = keep.tile([P, H], U32, name="wa_codes", align_bytes=64)
        wa_scales = keep.tile([P, H], U8, name="wa_scales", align_bytes=64)
        wa_bf = keep.tile([P, H, PACK], BF16, name="wa_bf", align_bytes=64)
        for u in range(2):
            nc.scalar.copy(woven(wa_bf[:, u * HALF : (u + 1) * HALF, :]), planes(wa_raw[u][:]))
        quantize(wa_codes[:], wa_scales[:], wa_bf[:])
        xa_words = keep.tile([P, S], U32, name="xa_words", align_bytes=64)
        nc.vector.tensor_copy(dealt(xa_words), table_words[:].bitcast(U32).indirect(offs_sb[:]))
        xb_scales = keep.tile([P, S], U8, name="xb_scales", align_bytes=64)
        nc.vector.tensor_copy(dealt(xb_scales), table_scales[:].indirect(two_sb[:]))

        identity = keep.tile([P, P], F32, name="identity")
        make_identity(nc, identity[:])
        turned = psum.tile([P, P], F32, name="turned", tag="rows0")
        nc.tensor.transpose(turned[:], place_rows[:], identity[:])
        by_place = keep.tile([P, 4 * PACK], F32, name="by_place")
        nc.scalar.copy(by_place[:], turned[:, : 4 * PACK])
        sl_sb, th_sb, gt_sb, gi_sb = [by_place[:, PACK * v : PACK * (v + 1)] for v in range(4)]
        bias1 = keep.tile([P, PACK], F32, name="bias1")
        nc.vector.scalar_tensor_tensor(bias1[:], sl_sb, -1.0, th_sb, MULT, MULT)

        a_sb = [keep.tile([P, H], F32, name=f"a_sb{j}") for j in range(PACK)]
        sg = [keep.tile([P, PACK, HALF], F32, name=f"sg{u}") for u in range(2)]
        other = [keep.tile([P, PACK, HALF], F32, name=f"other{u}") for u in range(2)]

        def look_up_in_a(u, j):
            nc.scalar.activation(
                sg[u][:, j, :],
                a_sb[j][:].indirect(entries(n1_sb, u * HALF, HALF)),
                SIGMOID,
                bias=bias1[:, j : j + 1],
                scale=sl_sb[:, j : j + 1],
            )
            nc.scalar.activation(
                other[u][:, j, :], a_sb[j][:].indirect(entries(n2_sb, u * HALF, HALF)), COPY, scale=0.75
            )

        for j in range(PACK):
            places = slice(j * P, (j + 1) * P)
            bank = psum.tile([P, H], F32, name=f"a_ps{j}", tag=f"rows{j}")
            nc.tensor.matmul_mx(
                out=bank[:],
                lhsT=xa_words[:, places].bitcast(FP8X4),
                lhsT_scale=xa_scales[:, places],
                rhs=wa_codes[:].bitcast(FP8X4),
                rhs_scale=wa_scales[:],
                start=True,
                stop=True,
            )
            if j < SCALAR_BANKS:
                nc.scalar.copy(a_sb[j][:], bank[:])
            else:
                nc.vector.tensor_copy(a_sb[j][:], bank[:])
            look_up_in_a(0, j)
        for j in range(PACK):
            look_up_in_a(1, j)

        xb_words = keep.tile([P, S], U32, name="xb_words", align_bytes=64)
        nc.vector.tensor_copy(dealt(xb_words), table_words[:].bitcast(U32).indirect(two_sb[:]))
        wb_bf = keep.tile([P, N, PACK], BF16, name="wb_bf", tag="after_wb", align_bytes=64)
        nc.vector.tensor_copy(woven(wb_bf[:]), planes(wb_raw[:]))
        wb_codes = keep.tile([P, N], U32, name="wb_codes", align_bytes=64)
        wb_scales = keep.tile([P, N], U8, name="wb_scales", align_bytes=64)
        quantize(wb_codes[:], wb_scales[:], wb_bf[:])
        z2_bf = keep.tile([P, N, PACK], BF16, name="z2_bf", align_bytes=64)
        for n in range(N // P):
            cols = slice(n * P, (n + 1) * P)
            bank = psum.tile([P, PACK, P], F32, name=f"b_ps{n}", tag=f"b_ps{n}")
            for j in range(PACK):
                places = slice(j * P, (j + 1) * P)
                nc.tensor.matmul_mx(
                    out=bank[:, j, :],
                    lhsT=xb_words[:, places].bitcast(FP8X4),
                    lhsT_scale=xb_scales[:, places],
                    rhs=wb_codes[:, cols].bitcast(FP8X4),
                    rhs_scale=wb_scales[:, cols],
                    start=True,
                    stop=True,
                )
            nc.vector.tensor_tensor(
                z2_bf[:, cols, :],
                bank[:].rearrange("p j c -> p c j"),
                gi_sb.unsqueeze(1).to_broadcast([P, P, PACK]),
                MULT,
            )
        z2_codes = keep.tile([P, N], U32, name="z2_codes", align_bytes=64)
        z2_scales = keep.tile([P, N], U8, name="z2_scales", align_bytes=64)
        quantize(z2_codes[:], z2_scales[:], z2_bf[:])

        bias2 = keep.tile([P, H // P], F32, name="bias2")
        nc.vector.scalar_tensor_tensor(bias2[:], sl2_sb[:], -1.0, th2_sb[:], MULT, MULT)
        scale3 = keep.tile([P, H // P], F32, name="scale3")
        nc.vector.tensor_scalar(scale3[:], sl3_sb[:], -1.0, None, MULT)
        bias3 = keep.tile([P, H // P], F32, name="bias3")
        nc.vector.tensor_tensor(bias3[:], sl3_sb[:], th3_sb[:], MULT)

        cv_sb = []
        windows = [keep.tile([P, 2 * N], F32, name=f"cv_window{m}") for m in range(H // P)]
        for window in windows:
            nc.gpsimd.memset(window[:, N:], 0.0)
        for m in range(H // P):
            u, start = divmod(m * P, HALF)
            part = slice(start, start + P)
            if start == 0:
                tag = "after_wb" if u == 0 else "after_z1"
                gated = keep.tile([P, PACK, HALF], F32, name=f"gated{u}", tag=tag, align_bytes=64)
                for j in range(PACK):
                    nc.vector.tensor_tensor(
                        gated[:, j, :], a_sb[j][:, u * HALF : (u + 1) * HALF], sg[u][:, j, :], MULT
                    )
            larger = keep.tile([P, PACK, P], F32, name=f"larger{m}")
            nc.vector.tensor_tensor(larger[:], gated[:, :, part], other[u][:, :, part], MAX)
            z_bf = keep.tile([P, P, PACK], BF16, name=f"z_bf{m}", tag=f"after_z{m}", align_bytes=64)
            nc.vector.tensor_tensor(
                woven(z_bf[:]),
                planes(larger[:]),
                gt_sb.unsqueeze(1).unsqueeze(3).to_broadcast([P, P // RUN, PACK, RUN]),
                MULT,
            )
            z_codes = keep.tile([P, P], U32, name=f"z_codes{m}", tag=f"after_cv{m}", align_bytes=64)
            z_scales = keep.tile([P, P], U8, name=f"z_scales{m}", align_bytes=64)
            quantize(z_codes[:], z_scales[:], z_bf[:])
            bank = psum.tile([P, N], F32, name=f"cv_ps{m}", tag=f"rows{m}")
            nc.tensor.matmul_mx(
                out=bank[:],
                lhsT=z_codes[:].bitcast(FP8X4),
                lhsT_scale=z_scales[:],
                rhs=z2_codes[:].bitcast(FP8X4),
                rhs_scale=z2_scales[:],
                start=True,
                stop=True,
            )
            cv_m = windows[m][:, :N]
            if m < SCALAR_BANKS:
                nc.scalar.activation(cv_m, bank[:], COPY, scale=0.0625)
            else:
                nc.vector.tensor_scalar(cv_m, bank[:], 0.0625, None, MULT)
            cv_sb.append(cv_m)

        last = H // P - 1
        twice_tags = ["after_z3", "after_cv3", "after_z3", "after_cv3"]
        for m in range(H // P):
            row = slice(m, m + 1)
            sg2 = keep.tile([P, N], F32, name=f"sg2_{m}")
            sg3 = keep.tile([P, N], F32, name=f"sg3_{m}")
            width = HALF if m == last else N
            for gate, feature_list, scale, bias in ((sg2, n3_sb, sl2_sb, bias2), (sg3, n4_sb, scale3, bias3)):
                step = width if gate is sg3 else N
                for c0 in range(0, N, step):
                    nc.scalar.activation(
                        gate[:, c0 : c0 + step],
                        windows[m][:].indirect(entries(feature_list, c0, step)),
                        SIGMOID,
                        bias=bias[:, row],
                        scale=scale[:, row],
                    )
            twice = keep.tile([P, N], F32, name=f"twice{m}", tag=twice_tags[m], align_bytes=64)
            nc.vector.scalar_tensor_tensor(twice[:], cv_sb[m], 2.0, sg2[:], MULT, MULT)
            for c0 in range(0, N, width):
                cols = slice(c0, c0 + width)
                result = keep.tile([P, width], F32, name=f"result{m}_{c0}")
                nc.vector.tensor_tensor(result[:], twice[:, cols], sg3[:, cols], MULT)
                nc.sync.dma_start(out[m * P : (m + 1) * P, cols], result[:])
